import numpy as np
import ml_dtypes


def mxq(x, axis, fmt="e4m3"):
    dtype, down = {"e4m3": (ml_dtypes.float8_e4m3fn, 7), "e5m2": (ml_dtypes.float8_e5m2, 14)}[fmt]
    v = np.moveaxis(np.asarray(x, np.float32).astype(ml_dtypes.bfloat16).astype(np.float64), axis, -1)
    blocks = v.reshape(v.shape[:-1] + (-1, 32))
    amax = np.abs(blocks).max(-1, keepdims=True)
    byte = np.maximum(np.where(amax > 0, np.frexp(amax)[1] - 1 + 127, 0) - down, 1)
    scale = np.exp2(byte - 127.0)
    codes = (blocks / scale).astype(np.float32).astype(dtype).astype(np.float64)
    return np.moveaxis((codes * scale).reshape(v.shape), -1, axis)


WIDE = False


def mx_kscale(k):
    if not WIDE:
        return np.ones(k)
    levels = np.array([30, -30])
    if k % 512:
        return np.exp2(np.random.permutation(np.resize(levels, k // 32))).repeat(32)
    a = np.empty((k // 512, 16))
    for p in range(k // 512):
        a[p, :8] = np.random.permutation(np.resize(levels, 8))
        for g in range(8):
            far = levels[np.abs(levels - a[p, g]) >= 10]
            a[p, g + 8] = far[np.random.randint(len(far))]
    return np.exp2(a.ravel()).repeat(32)


def f64(x):
    return np.asarray(x).astype(np.float64)


E2M1 = np.array([0.0, 0.5, 1.0, 1.5, 2.0, 3.0, 4.0, 6.0, -0.0, -0.5, -1.0, -1.5, -2.0, -3.0, -4.0, -6.0])


def pack_weight(w, fmt):
    k, n = w.shape
    w = f64(np.asarray(w, np.float32).astype(ml_dtypes.bfloat16)).reshape(k // 32, 32, n)
    amax = np.abs(w).max(1)
    if fmt == "e4m3":
        byte = np.frexp(amax)[1] - 1 + 127 - 7
    else:
        mant, ex = np.frexp(amax / 6.0)
        byte = np.where(mant > 0.5, ex, ex - 1) + 127
    byte = np.clip(np.where(amax > 0, byte, 1), 1, 254)
    scaled = (w * np.exp2(127.0 - byte)[:, None, :]).reshape(k, n).astype(np.float32)
    by_word = np.ascontiguousarray(scaled.reshape(k // 512, 128, 4, n).transpose(0, 1, 3, 2))
    if fmt == "e4m3":
        words = by_word.astype(ml_dtypes.float8_e4m3fn).view(np.uint8)
    else:
        c = by_word.astype(ml_dtypes.float4_e2m1fn).view(np.uint8) & 0xF
        words = (c[..., 0::2] | (c[..., 1::2] << 4)).reshape(k // 512, 128, 2 * n)
    return np.ascontiguousarray(words), np.ascontiguousarray(byte.astype(np.uint8).reshape(k // 512, 16, n))


def unpack_weight(words, scales, fmt):
    g, _, n = scales.shape
    words = np.ascontiguousarray(words).reshape(g, 128, n, -1)
    if fmt == "e4m3":
        vals = words.view(ml_dtypes.float8_e4m3fn).astype(np.float64)
    else:
        nib = np.empty((g, 128, n, 4), np.uint8)
        nib[..., 0::2] = words & 0xF
        nib[..., 1::2] = words >> 4
        vals = E2M1[nib]
    vals = vals * np.repeat(np.exp2(scales.astype(np.float64) - 127.0), 8, axis=1)[..., None]
    return vals.transpose(0, 1, 3, 2).reshape(g * 512, n)


def bf(x):
    return np.asarray(x, np.float32).astype(ml_dtypes.bfloat16)


def planes(Y):
    r, m = Y.shape
    b = f64(bf(Y)).reshape(r // 32, 32, m)
    amax = np.abs(b).max(1)
    byte = np.clip(np.where(amax > 0, np.frexp(amax)[1] - 1 + 127 - 7, 1), 1, 254)
    codes = (b * np.exp2(127.0 - byte)[:, None, :]).reshape(r, m).astype(np.float32).astype(ml_dtypes.float8_e4m3fn).view(np.uint8)
    words = codes.reshape(r // 512, 128, 4, m).transpose(0, 1, 3, 2)
    return np.ascontiguousarray(words), np.ascontiguousarray(byte.astype(np.uint8).reshape(r // 512, 16, m))


K, T, N = 1024, 512, 512


def setup_inputs():
    n = np.random.standard_normal
    fk = mx_kscale(K)
    wap = pack_weight(n((K, N)) * 1 / np.sqrt(K) * fk[:, None], "e4m3")
    wbp = pack_weight(n((K, N)) * 1 / np.sqrt(K) * fk[:, None], "e2m1")
    return {
        "xf": (n((K, T))).astype(np.float32),
        "fa": (np.random.uniform(0.5, 2.0, (K, 1)) / fk[:, None]).astype(np.float32),
        "fb": (np.random.uniform(0.5, 2.0, (K, 1)) / fk[:, None]).astype(np.float32),
        "wa_words": wap[0],
        "wa_scales": wap[1],
        "wb_words": wbp[0],
        "wb_scales": wbp[1],
    }


def reference(xf, fa, fb, wa_words, wa_scales, wb_words, wb_scales):
    wau = unpack_weight(wa_words, wa_scales, "e4m3")
    wbu = unpack_weight(wb_words, wb_scales, "e2m1")
    x1 = np.pad(f64(xf), ((0, 0), (1, 0)))[:, :T]
    x2 = np.pad(f64(xf), ((0, 0), (2, 0)))[:, :T]
    m = np.maximum(x1, x2)
    ua = np.maximum(f64(xf) - m, 0.0) * f64(fa)
    ub = np.maximum(m - f64(xf), 0.0) * f64(fb)
    uaq = mxq(ua, 0, "e5m2")
    ubq = mxq(ub, 0, "e4m3")
    y = wau.T @ uaq + wbu.T @ ubq
    words, scales = planes(y)
    return y, words, scales

@@ -1,0 +1,230 @@
+from contextlib import ExitStack
+
+import concourse.mybir as mybir
+from concourse.masks import make_identity
+
+K, T, N = 1024, 512, 512
+FLOPS = 2 * 2 * K * T * N
+
+F32 = mybir.dt.float32
+BF16 = mybir.dt.bfloat16
+I32 = mybir.dt.int32
+U32 = mybir.dt.uint32
+U8 = mybir.dt.uint8
+E4M3 = mybir.dt.float8_e4m3fn_x4
+E5M2 = mybir.dt.float8_e5m2_x4
+E2M1 = mybir.dt.float4_e2m1fn_x4
+ALU = mybir.AluOpType
+ACT = mybir.ActivationFunctionType
+
+P = 128
+PACK = 4
+PASSES = K // (P * PACK)
+TILE = 128
+TILES = T // TILE
+PAD = 8
+RUN = 4
+
+
+def tile_mix_ahead_and_behind_pl_kernel(
+    tc, xf, fa, fb, wa_words, wa_scales, wb_words, wb_scales, out_0, out_1, out_2
+):
+    nc = tc.nc
+    steps = [(c, z) for c in range(TILES) for z in range(PASSES)]
+    last = len(steps) - 1
+
+    with ExitStack() as ctx:
+        sb = ctx.enter_context(tc.tile_pool(name="sb", bufs=1))
+        ps = ctx.enter_context(tc.psum_pool(name="ps", bufs=1))
+        ctx.enter_context(tc.manual_schedule())
+
+        x_hbm = xf.rearrange("(z p j) t -> z p j t", z=PASSES, j=PACK)
+        x_sb = [sb.tile([P, PACK, PAD + T], F32, name="x%d" % z) for z in range(PASSES)]
+        fa_sb = sb.tile([P, PASSES, PACK], F32)
+        fb_sb = sb.tile([P, PASSES, PACK], F32)
+        neg_fb = sb.tile([P, PASSES, PACK], F32)
+        wa_sb = sb.tile([P, PASSES, N], U32, align_bytes=64)
+        wb_sb = sb.tile([P, PASSES, 2 * N], U8, align_bytes=64)
+        wa_plane = sb.tile([P, PASSES, N], U8, align_bytes=64)
+        wb_plane = sb.tile([P, PASSES, N], U8, align_bytes=64)
+        identity = sb.tile([P, P], F32)
+        y_plane = sb.tile([P, T], U8, align_bytes=64)
+
+        def load_x(s):
+            c, z = steps[s]
+            nc.sync.dma_start(
+                out=x_sb[z][:, :, PAD + c * TILE : PAD + (c + 1) * TILE],
+                in_=x_hbm[z][:, :, c * TILE : (c + 1) * TILE],
+            )
+
+        def load_plane(plane, scales):
+            for q in range(4):
+                nc.sync.dma_start(
+                    out=plane[32 * q : 32 * q + 4, :, :].bitcast(I32),
+                    in_=scales[:, 4 * q : 4 * q + 4, :].rearrange("z r n -> r z n").bitcast(I32),
+                )
+
+        for z in range(PASSES):
+            nc.vector.memset(x_sb[z][:, :, 0:PAD], 0.0)
+        for plane in (wa_plane, wb_plane):
+            nc.vector.memset(plane[:].bitcast(I32), 0)
+        make_identity(nc, identity[:])
+
+        load_x(0)
+        nc.scalar.dma_start(out=fb_sb[:], in_=fb.rearrange("(z p j) o -> p z (j o)", z=PASSES, j=PACK))
+        nc.scalar.dma_start(out=fa_sb[:], in_=fa.rearrange("(z p j) o -> p z (j o)", z=PASSES, j=PACK))
+        load_x(1)
+        load_x(2)
+        nc.sync.dma_start(out=wa_sb[:].bitcast(I32), in_=wa_words.rearrange("z p n r -> p z (n r)").bitcast(I32))
+        nc.sync.dma_start(out=wb_sb[:].bitcast(I32), in_=wb_words.rearrange("z p b -> p z b").bitcast(I32))
+        load_plane(wa_plane, wa_scales)
+        load_plane(wb_plane, wb_scales)
+        for s in range(3, len(steps)):
+            load_x(s)
+
+        nc.scalar.activation(out=neg_fb[:], in_=fb_sb[:], func=ACT.Copy, scale=-1.0)
+
+        peak, diff, rows, packed, codes, planes = {}, {}, {}, {}, {}, {}
+        acc, y_t, y_ps, y_bf = {}, {}, {}, {}
+
+        def take_peak(s):
+            c, z = steps[s]
+            t0 = PAD + c * TILE
+            peak[s] = sb.tile([P, PACK, TILE], F32, name="peak%d" % s)
+            nc.vector.tensor_tensor(
+                out=peak[s][:],
+                in0=x_sb[z][:, :, t0 - 1 : t0 - 1 + TILE],
+                in1=x_sb[z][:, :, t0 - 2 : t0 - 2 + TILE],
+                op=ALU.max,
+            )
+
+        def take_diff(s):
+            c, z = steps[s]
+            t0 = PAD + c * TILE
+            diff[s] = sb.tile([P, PACK, TILE], F32, name="diff%d" % s)
+            nc.vector.tensor_tensor(
+                out=diff[s][:], in0=x_sb[z][:, :, t0 : t0 + TILE], in1=peak[s][:], op=ALU.subtract
+            )
+
+        def scale_rows(s, side):
+            z = steps[s][1]
+            clip, factor = ((ALU.max, fa_sb), (ALU.min, neg_fb))[side]
+            rows[s, side] = sb.tile([P, PACK, TILE], BF16, name="rows%d_%d" % (s, side))
+            for j in range(PACK):
+                nc.vector.tensor_scalar(
+                    out=rows[s, side][:, j, :],
+                    in0=diff[s][:, j, :],
+                    scalar1=0.0,
+                    scalar2=factor[:, z, j : j + 1],
+                    op0=clip,
+                    op1=ALU.mult,
+                )
+
+        def interleave(s, side, copy):
+            packed[s, side] = sb.tile([P, TILE, PACK], BF16, name="packed%d_%d" % (s, side), align_bytes=64)
+            copy(
+                out=packed[s, side][:].rearrange("p (c i) j -> p c j i", i=RUN),
+                in_=rows[s, side][:].rearrange("p j (c i) -> p c j i", i=RUN),
+            )
+
+        def quantize(s, side):
+            codes[s, side] = sb.tile([P, TILE], U32, name="codes%d_%d" % (s, side), align_bytes=64)
+            planes[s, side] = sb.tile([P, TILE], U8, name="plane%d_%d" % (s, side), align_bytes=64)
+            nc.vector.quantize_mx(
+                out=codes[s, side][:].bitcast((E5M2, E4M3)[side]),
+                scales=planes[s, side][:],
+                in_=packed[s, side][:].rearrange("p t j -> p (t j)"),
+            )
+
+        def multiply(s):
+            c, z = steps[s]
+            if z == 0:
+                acc[c] = ps.tile([P, N], F32, name="acc%d" % c)
+            nc.tensor.matmul_mx(
+                out=acc[c][:],
+                lhsT=codes[s, 0][:].bitcast(E5M2),
+                lhsT_scale=planes[s, 0][:],
+                rhs=wa_sb[:, z, :].bitcast(E4M3),
+                rhs_scale=wa_plane[:, z, :],
+                start=(z == 0),
+                stop=False,
+            )
+            nc.tensor.matmul_mx(
+                out=acc[c][:],
+                lhsT=codes[s, 1][:].bitcast(E4M3),
+                lhsT_scale=planes[s, 1][:],
+                rhs=wb_sb[:, z, :].bitcast(E2M1),
+                rhs_scale=wb_plane[:, z, :],
+                start=False,
+                stop=(z == PASSES - 1),
+            )
+
+        def turn(c):
+            y_t[c] = sb.tile([P, PACK, P], F32, name="y_t%d" % c)
+            nc.scalar.copy(out=y_t[c][:], in_=acc[c][:].rearrange("t (p i) -> t i p", i=PACK))
+            y_ps[c] = ps.tile([P, PACK, TILE], F32, name="y_ps%d" % c)
+            for i in range(PACK):
+                nc.tensor.transpose(y_ps[c][:, i, :], y_t[c][:, i, :], identity[:])
+
+        def round_result(c, copy):
+            y_bf[c] = sb.tile([P, TILE, PACK], BF16, name="y_bf%d" % c, align_bytes=64)
+            copy(out=y_bf[c][:], in_=y_ps[c][:].rearrange("p i t -> p t i"))
+
+        def store_result(c):
+            y_sb = sb.tile([P, PACK, TILE], F32, name="y_sb%d" % c)
+            nc.scalar.copy(out=y_sb[:], in_=y_ps[c][:])
+            nc.sync.dma_start(
+                out=out_0.rearrange("(p i) t -> p i t", i=PACK)[:, :, c * TILE : (c + 1) * TILE], in_=y_sb[:]
+            )
+
+        def store_words(c):
+            y_codes = sb.tile([P, TILE], U32, name="y_codes%d" % c, align_bytes=64)
+            nc.vector.quantize_mx(
+                out=y_codes[:].bitcast(E4M3),
+                scales=y_plane[:, c * TILE : (c + 1) * TILE],
+                in_=y_bf[c][:].rearrange("p t i -> p (t i)"),
+            )
+            nc.sync.dma_start(
+                out=out_1[0].rearrange("p t r -> p (t r)").bitcast(I32)[:, c * TILE : (c + 1) * TILE],
+                in_=y_codes[:].bitcast(I32),
+            )
+
+        take_peak(0)
+        for s in range(len(steps)):
+            take_diff(s)
+            if s < last:
+                take_peak(s + 1)
+            if s >= 3 and s % 2 == 1:
+                turn((s - 3) // 2)
+            if s >= 4 and s % 2 == 0:
+                round_result((s - 4) // 2, nc.scalar.copy)
+                store_result((s - 4) // 2)
+            if s >= 1:
+                quantize(s - 1, 0)
+                quantize(s - 1, 1)
+                multiply(s - 1)
+            if s >= 5 and s % 2 == 1:
+                store_words((s - 5) // 2)
+            scale_rows(s, 0)
+            interleave(s, 0, nc.scalar.copy)
+            scale_rows(s, 1)
+            if s < last:
+                interleave(s, 1, nc.scalar.copy)
+
+        interleave(last, 1, nc.vector.tensor_copy)
+        quantize(last, 0)
+        quantize(last, 1)
+        multiply(last)
+        round_result(TILES - 2, nc.scalar.copy)
+        store_result(TILES - 2)
+        store_words(TILES - 2)
+        turn(TILES - 1)
+        round_result(TILES - 1, nc.vector.tensor_copy)
+        store_result(TILES - 1)
+        store_words(TILES - 1)
+        for q in range(4):
+            queue = (nc.scalar, nc.sync)[q % 2]
+            queue.dma_start(
+                out=out_2[0][4 * q : 4 * q + 4, :].bitcast(I32),
+                in_=y_plane[32 * q : 32 * q + 4, :].bitcast(I32),
+            )

@@ -24,6 +24,8 @@ TILE = 128
 TILES = T // TILE
 PAD = 8
 RUN = 4
+ALL = slice(0, PACK)
+PAIRS = (slice(0, 2), slice(2, 4))
 
 
 def tile_mix_ahead_and_behind_pl_kernel(
@@ -50,11 +52,11 @@ def tile_mix_ahead_and_behind_pl_kernel(
         identity = sb.tile([P, P], F32)
         y_plane = sb.tile([P, T], U8, align_bytes=64)
 
-        def load_x(s):
+        def load_x(s, js=ALL):
             c, z = steps[s]
             nc.sync.dma_start(
-                out=x_sb[z][:, :, PAD + c * TILE : PAD + (c + 1) * TILE],
-                in_=x_hbm[z][:, :, c * TILE : (c + 1) * TILE],
+                out=x_sb[z][:, js, PAD + c * TILE : PAD + (c + 1) * TILE],
+                in_=x_hbm[z][:, js, c * TILE : (c + 1) * TILE],
             )
 
         def load_plane(plane, scales):
@@ -70,40 +72,42 @@ def tile_mix_ahead_and_behind_pl_kernel(
             nc.vector.memset(plane[:].bitcast(I32), 0)
         make_identity(nc, identity[:])
 
-        load_x(0)
-        nc.scalar.dma_start(out=fb_sb[:], in_=fb.rearrange("(z p j) o -> p z (j o)", z=PASSES, j=PACK))
-        nc.scalar.dma_start(out=fa_sb[:], in_=fa.rearrange("(z p j) o -> p z (j o)", z=PASSES, j=PACK))
+        for js in PAIRS:
+            load_x(0, js)
+        nc.sync.dma_start(out=fb_sb[:], in_=fb.rearrange("(z p j) o -> p z (j o)", z=PASSES, j=PACK))
+        nc.sync.dma_start(out=fa_sb[:], in_=fa.rearrange("(z p j) o -> p z (j o)", z=PASSES, j=PACK))
         load_x(1)
         load_x(2)
+        load_x(3)
         nc.sync.dma_start(out=wa_sb[:].bitcast(I32), in_=wa_words.rearrange("z p n r -> p z (n r)").bitcast(I32))
         nc.sync.dma_start(out=wb_sb[:].bitcast(I32), in_=wb_words.rearrange("z p b -> p z b").bitcast(I32))
         load_plane(wa_plane, wa_scales)
         load_plane(wb_plane, wb_scales)
-        for s in range(3, len(steps)):
+        for s in range(4, len(steps)):
             load_x(s)
 
         nc.scalar.activation(out=neg_fb[:], in_=fb_sb[:], func=ACT.Copy, scale=-1.0)
 
-        peak, diff, rows, packed, codes, planes = {}, {}, {}, {}, {}, {}
+        peak = [sb.tile([P, PACK, TILE], F32, name="peak%d" % s) for s in range(len(steps))]
+        diff = [sb.tile([P, PACK, TILE], F32, name="diff%d" % s) for s in range(len(steps))]
+        rows, packed, codes, planes = {}, {}, {}, {}
         acc, y_t, y_ps, y_bf = {}, {}, {}, {}
 
-        def take_peak(s):
+        def take_peak(s, js=ALL):
             c, z = steps[s]
             t0 = PAD + c * TILE
-            peak[s] = sb.tile([P, PACK, TILE], F32, name="peak%d" % s)
             nc.vector.tensor_tensor(
-                out=peak[s][:],
-                in0=x_sb[z][:, :, t0 - 1 : t0 - 1 + TILE],
-                in1=x_sb[z][:, :, t0 - 2 : t0 - 2 + TILE],
+                out=peak[s][:, js, :],
+                in0=x_sb[z][:, js, t0 - 1 : t0 - 1 + TILE],
+                in1=x_sb[z][:, js, t0 - 2 : t0 - 2 + TILE],
                 op=ALU.max,
             )
 
-        def take_diff(s):
+        def take_diff(s, js=ALL):
             c, z = steps[s]
             t0 = PAD + c * TILE
-            diff[s] = sb.tile([P, PACK, TILE], F32, name="diff%d" % s)
             nc.vector.tensor_tensor(
-                out=diff[s][:], in0=x_sb[z][:, :, t0 : t0 + TILE], in1=peak[s][:], op=ALU.subtract
+                out=diff[s][:, js, :], in0=x_sb[z][:, js, t0 : t0 + TILE], in1=peak[s][:, js, :], op=ALU.subtract
             )
 
         def scale_rows(s, side):
@@ -159,22 +163,35 @@ def tile_mix_ahead_and_behind_pl_kernel(
                 stop=(z == PASSES - 1),
             )
 
-        def turn(c):
+        y_hbm = out_0.rearrange("(p i) t -> p i t", i=PACK)
+        y_sb = [sb.tile([P, PACK, TILE], F32, name="y_sb%d" % c) for c in range(TILES)]
+
+        def drain(c, pieces=(ALL,)):
             y_t[c] = sb.tile([P, PACK, P], F32, name="y_t%d" % c)
-            nc.scalar.copy(out=y_t[c][:], in_=acc[c][:].rearrange("t (p i) -> t i p", i=PACK))
-            y_ps[c] = ps.tile([P, PACK, TILE], F32, name="y_ps%d" % c)
-            for i in range(PACK):
-                nc.tensor.transpose(y_ps[c][:, i, :], y_t[c][:, i, :], identity[:])
+            dealt = acc[c][:].rearrange("t (p i) -> t i p", i=PACK)
+            for part in pieces:
+                nc.scalar.copy(out=y_t[c][:, part, :], in_=dealt[:, part, :])
 
-        def round_result(c, copy):
+        def turn(c, part=ALL):
+            count = part.stop - part.start
+            bank = ps.tile([P, count, TILE], F32, name="y_ps%d_%d" % (c, part.start), tag="turned", bufs=4)
+            for i in range(count):
+                nc.tensor.transpose(bank[:, i, :], y_t[c][:, part.start + i, :], identity[:])
+            y_ps[c, part.start] = bank
+
+        def store_result(c, copy, queue, part=ALL):
+            copy(out=y_sb[c][:, part, :], in_=y_ps[c, part.start][:])
+            queue.dma_start(out=y_hbm[:, part, c * TILE : (c + 1) * TILE], in_=y_sb[c][:, part, :])
+
+        def round_from_psum(c):
             y_bf[c] = sb.tile([P, TILE, PACK], BF16, name="y_bf%d" % c, align_bytes=64)
-            copy(out=y_bf[c][:], in_=y_ps[c][:].rearrange("p i t -> p t i"))
+            nc.scalar.copy(out=y_bf[c][:], in_=y_ps[c, 0][:].rearrange("p i t -> p t i"))
 
-        def store_result(c):
-            y_sb = sb.tile([P, PACK, TILE], F32, name="y_sb%d" % c)
-            nc.scalar.copy(out=y_sb[:], in_=y_ps[c][:])
-            nc.sync.dma_start(
-                out=out_0.rearrange("(p i) t -> p i t", i=PACK)[:, :, c * TILE : (c + 1) * TILE], in_=y_sb[:]
+        def round_from_sbuf(c):
+            y_bf[c] = sb.tile([P, TILE, PACK], BF16, name="y_bf%d" % c, align_bytes=64)
+            nc.vector.tensor_copy(
+                out=y_bf[c][:].rearrange("p (c i) j -> p c j i", i=RUN),
+                in_=y_sb[c][:].rearrange("p j (c i) -> p c j i", i=RUN),
             )
 
         def store_words(c):
@@ -189,41 +206,61 @@ def tile_mix_ahead_and_behind_pl_kernel(
                 in_=y_codes[:].bitcast(I32),
             )
 
-        take_peak(0)
-        for s in range(len(steps)):
+        for js in PAIRS:
+            take_peak(0, js)
+        for js in PAIRS:
+            take_diff(0, js)
+        scale_rows(0, 0)
+        interleave(0, 0, nc.scalar.copy)
+        take_peak(1)
+        scale_rows(0, 1)
+        interleave(0, 1, nc.scalar.copy)
+
+        for s in range(1, last):
             take_diff(s)
-            if s < last:
-                take_peak(s + 1)
-            if s >= 3 and s % 2 == 1:
-                turn((s - 3) // 2)
-            if s >= 4 and s % 2 == 0:
-                round_result((s - 4) // 2, nc.scalar.copy)
-                store_result((s - 4) // 2)
-            if s >= 1:
-                quantize(s - 1, 0)
-                quantize(s - 1, 1)
-                multiply(s - 1)
-            if s >= 5 and s % 2 == 1:
-                store_words((s - 5) // 2)
+            take_peak(s + 1)
+            quantize(s - 1, 0)
             scale_rows(s, 0)
             interleave(s, 0, nc.scalar.copy)
+            quantize(s - 1, 1)
+            multiply(s - 1)
             scale_rows(s, 1)
-            if s < last:
-                interleave(s, 1, nc.scalar.copy)
+            interleave(s, 1, nc.scalar.copy)
+            if s % 2 == 0:
+                drain(s // 2 - 1)
+                if s + 1 < last:
+                    turn(s // 2 - 1)
+            elif s >= 3:
+                store_result((s - 3) // 2, nc.scalar.copy, nc.sync)
+                round_from_psum((s - 3) // 2)
+            if s == 5:
+                store_words(0)
 
+        take_diff(last)
+        quantize(last - 1, 0)
+        scale_rows(last, 0)
+        interleave(last, 0, nc.scalar.copy)
+        quantize(last - 1, 1)
+        multiply(last - 1)
+        turn(TILES - 2)
+        scale_rows(last, 1)
         interleave(last, 1, nc.vector.tensor_copy)
         quantize(last, 0)
         quantize(last, 1)
         multiply(last)
-        round_result(TILES - 2, nc.scalar.copy)
-        store_result(TILES - 2)
+        store_result(TILES - 2, nc.scalar.copy, nc.sync)
+        store_words(TILES - 3)
+        round_from_sbuf(TILES - 2)
         store_words(TILES - 2)
-        turn(TILES - 1)
-        round_result(TILES - 1, nc.vector.tensor_copy)
-        store_result(TILES - 1)
+        drain(TILES - 1, [slice(i, i + 1) for i in range(PACK)])
+        for part in PAIRS:
+            turn(TILES - 1, part)
+        store_result(TILES - 1, nc.scalar.copy, nc.scalar, PAIRS[0])
+        store_result(TILES - 1, nc.vector.tensor_copy, nc.sync, PAIRS[1])
+        round_from_sbuf(TILES - 1)
         store_words(TILES - 1)
         for q in range(4):
-            queue = (nc.scalar, nc.sync)[q % 2]
+            queue = (nc.sync, nc.scalar)[q % 2]
             queue.dma_start(
                 out=out_2[0][4 * q : 4 * q + 4, :].bitcast(I32),
                 in_=y_plane[32 * q : 32 * q + 4, :].bitcast(I32),

@@ -24,6 +24,7 @@ TILE = 128
 TILES = T // TILE
 PAD = 8
 RUN = 4
+SHARED = 3
 ALL = slice(0, PACK)
 PAIRS = (slice(0, 2), slice(2, 4))
 
@@ -76,14 +77,13 @@ def tile_mix_ahead_and_behind_pl_kernel(
             load_x(0, js)
         nc.sync.dma_start(out=fb_sb[:], in_=fb.rearrange("(z p j) o -> p z (j o)", z=PASSES, j=PACK))
         nc.sync.dma_start(out=fa_sb[:], in_=fa.rearrange("(z p j) o -> p z (j o)", z=PASSES, j=PACK))
-        load_x(1)
-        load_x(2)
-        load_x(3)
+        for s in range(1, len(steps) - PASSES):
+            load_x(s)
         nc.sync.dma_start(out=wa_sb[:].bitcast(I32), in_=wa_words.rearrange("z p n r -> p z (n r)").bitcast(I32))
         nc.sync.dma_start(out=wb_sb[:].bitcast(I32), in_=wb_words.rearrange("z p b -> p z b").bitcast(I32))
         load_plane(wa_plane, wa_scales)
         load_plane(wb_plane, wb_scales)
-        for s in range(4, len(steps)):
+        for s in range(len(steps) - PASSES, len(steps)):
             load_x(s)
 
         nc.scalar.activation(out=neg_fb[:], in_=fb_sb[:], func=ACT.Copy, scale=-1.0)
@@ -91,7 +91,7 @@ def tile_mix_ahead_and_behind_pl_kernel(
         peak = [sb.tile([P, PACK, TILE], F32, name="peak%d" % s) for s in range(len(steps))]
         diff = [sb.tile([P, PACK, TILE], F32, name="diff%d" % s) for s in range(len(steps))]
         rows, packed, codes, planes = {}, {}, {}, {}
-        acc, y_t, y_ps, y_bf = {}, {}, {}, {}
+        acc, y_t, y_ps = {}, {}, {}
 
         def take_peak(s, js=ALL):
             c, z = steps[s]
@@ -122,6 +122,19 @@ def tile_mix_ahead_and_behind_pl_kernel(
                     scalar2=factor[:, z, j : j + 1],
                     op0=clip,
                     op1=ALU.mult,
+                )
+
+        short = [sb.tile([P, PACK, TILE], F32, name="short%d" % s) for s in range(SHARED)]
+
+        def clip_on_scalar(s):
+            nc.scalar.activation(out=short[s][:], in_=diff[s][:], func=ACT.Relu, scale=-1.0)
+
+        def scale_rows_on_scalar(s):
+            z = steps[s][1]
+            rows[s, 1] = sb.tile([P, PACK, TILE], BF16, name="rows%d_1" % s)
+            for j in range(PACK):
+                nc.scalar.activation(
+                    out=rows[s, 1][:, j, :], in_=short[s][:, j, :], func=ACT.Copy, scale=fb_sb[:, z, j : j + 1]
                 )
 
         def interleave(s, side, copy):
@@ -183,82 +196,95 @@ def tile_mix_ahead_and_behind_pl_kernel(
             copy(out=y_sb[c][:, part, :], in_=y_ps[c, part.start][:])
             queue.dma_start(out=y_hbm[:, part, c * TILE : (c + 1) * TILE], in_=y_sb[c][:, part, :])
 
-        def round_from_psum(c):
-            y_bf[c] = sb.tile([P, TILE, PACK], BF16, name="y_bf%d" % c, align_bytes=64)
-            nc.scalar.copy(out=y_bf[c][:], in_=y_ps[c, 0][:].rearrange("p i t -> p t i"))
+        y_bf = sb.tile([P, T, PACK], BF16, align_bytes=64)
+        y_codes = sb.tile([P, T], U32, align_bytes=64)
+        words_hbm = out_1[0].rearrange("p t r -> p (t r)").bitcast(I32)
 
         def round_from_sbuf(c):
-            y_bf[c] = sb.tile([P, TILE, PACK], BF16, name="y_bf%d" % c, align_bytes=64)
             nc.vector.tensor_copy(
-                out=y_bf[c][:].rearrange("p (c i) j -> p c j i", i=RUN),
+                out=y_bf[:, c * TILE : (c + 1) * TILE, :].rearrange("p (c i) j -> p c j i", i=RUN),
                 in_=y_sb[c][:].rearrange("p j (c i) -> p c j i", i=RUN),
             )
 
-        def store_words(c):
-            y_codes = sb.tile([P, TILE], U32, name="y_codes%d" % c, align_bytes=64)
+        def quantize_result(first, count):
+            tokens = slice(first * TILE, (first + count) * TILE)
             nc.vector.quantize_mx(
-                out=y_codes[:].bitcast(E4M3),
-                scales=y_plane[:, c * TILE : (c + 1) * TILE],
-                in_=y_bf[c][:].rearrange("p t i -> p (t i)"),
+                out=y_codes[:, tokens].bitcast(E4M3),
+                scales=y_plane[:, tokens],
+                in_=y_bf[:, tokens, :].rearrange("p t i -> p (t i)"),
             )
-            nc.sync.dma_start(
-                out=out_1[0].rearrange("p t r -> p (t r)").bitcast(I32)[:, c * TILE : (c + 1) * TILE],
-                in_=y_codes[:].bitcast(I32),
-            )
+
+        def store_words(first, count):
+            tokens = slice(first * TILE, (first + count) * TILE)
+            nc.sync.dma_start(out=words_hbm[:, tokens], in_=y_codes[:, tokens].bitcast(I32))
+
+        def quantize_and_multiply(s):
+            quantize(s, 0)
+            quantize(s, 1)
+            multiply(s)
 
         for js in PAIRS:
             take_peak(0, js)
         for js in PAIRS:
             take_diff(0, js)
-        scale_rows(0, 0)
-        interleave(0, 0, nc.scalar.copy)
-        take_peak(1)
-        scale_rows(0, 1)
-        interleave(0, 1, nc.scalar.copy)
-
-        for s in range(1, last):
-            take_diff(s)
+        for s in range(last - 1):
+            if s > 0:
+                take_diff(s)
             take_peak(s + 1)
+            if s == 5:
+                drain(0)
+                turn(0)
+                quantize_and_multiply(3)
+            if s < SHARED:
+                clip_on_scalar(s)
+                if s > 0:
+                    interleave(s - 1, 1, nc.scalar.copy)
+                scale_rows_on_scalar(s)
+            scale_rows(s, 0)
+            interleave(s, 0, nc.scalar.copy)
+            if s >= SHARED:
+                scale_rows(s, 1)
+            if s >= SHARED - 1:
+                interleave(s, 1, nc.scalar.copy)
+            if s == 5:
+                quantize_and_multiply(4)
+            elif s >= 2:
+                quantize_and_multiply(s - 2)
+        store_result(0, nc.scalar.copy, nc.sync)
+        drain(1)
+
+        for s in (last - 1, last):
+            take_diff(s)
+            if s < last:
+                take_peak(s + 1)
             quantize(s - 1, 0)
             scale_rows(s, 0)
             interleave(s, 0, nc.scalar.copy)
             quantize(s - 1, 1)
             multiply(s - 1)
+            turn(s - 5)
             scale_rows(s, 1)
-            interleave(s, 1, nc.scalar.copy)
-            if s % 2 == 0:
-                drain(s // 2 - 1)
-                if s + 1 < last:
-                    turn(s // 2 - 1)
-            elif s >= 3:
-                store_result((s - 3) // 2, nc.scalar.copy, nc.sync)
-                round_from_psum((s - 3) // 2)
-            if s == 5:
-                store_words(0)
-
-        take_diff(last)
-        quantize(last - 1, 0)
-        scale_rows(last, 0)
-        interleave(last, 0, nc.scalar.copy)
-        quantize(last - 1, 1)
-        multiply(last - 1)
-        turn(TILES - 2)
-        scale_rows(last, 1)
+            if s < last:
+                interleave(s, 1, nc.scalar.copy)
+                drain(2)
         interleave(last, 1, nc.vector.tensor_copy)
-        quantize(last, 0)
-        quantize(last, 1)
-        multiply(last)
-        store_result(TILES - 2, nc.scalar.copy, nc.sync)
-        store_words(TILES - 3)
-        round_from_sbuf(TILES - 2)
-        store_words(TILES - 2)
+        quantize_and_multiply(last)
+        store_result(1, nc.scalar.copy, nc.sync)
+        for c in (0, 1):
+            round_from_sbuf(c)
+        store_result(2, nc.scalar.copy, nc.sync)
+        quantize_result(0, 2)
+        round_from_sbuf(2)
+        quantize_result(2, 1)
+        store_words(0, 3)
         drain(TILES - 1, [slice(i, i + 1) for i in range(PACK)])
         for part in PAIRS:
             turn(TILES - 1, part)
         store_result(TILES - 1, nc.scalar.copy, nc.scalar, PAIRS[0])
         store_result(TILES - 1, nc.vector.tensor_copy, nc.sync, PAIRS[1])
         round_from_sbuf(TILES - 1)
-        store_words(TILES - 1)
+        quantize_result(TILES - 1, 1)
+        store_words(TILES - 1, 1)
         for q in range(4):
             queue = (nc.sync, nc.scalar)[q % 2]
             queue.dma_start(

@@ -22,19 +22,22 @@ PACK = 4
 PASSES = K // (P * PACK)
 TILE = 128
 TILES = T // TILE
+QUADRANTS = 4
 PAD = 8
 RUN = 4
-SHARED = 3
+AHEAD, BEHIND = 0, 1
+BOTH = slice(0, 2)
 ALL = slice(0, PACK)
 PAIRS = (slice(0, 2), slice(2, 4))
+
+RANGES = ((0, TILE), (TILE, 2 * TILE), (3 * TILE, TILE))
+STEPS = [(z, first, count) for first, count in RANGES for z in range(PASSES)]
 
 
 def tile_mix_ahead_and_behind_pl_kernel(
     tc, xf, fa, fb, wa_words, wa_scales, wb_words, wb_scales, out_0, out_1, out_2
 ):
     nc = tc.nc
-    steps = [(c, z) for c in range(TILES) for z in range(PASSES)]
-    last = len(steps) - 1
 
     with ExitStack() as ctx:
         sb = ctx.enter_context(tc.tile_pool(name="sb", bufs=1))
@@ -42,6 +45,9 @@ def tile_mix_ahead_and_behind_pl_kernel(
         ctx.enter_context(tc.manual_schedule())
 
         x_hbm = xf.rearrange("(z p j) t -> z p j t", z=PASSES, j=PACK)
+        y_hbm = out_0.rearrange("(p i) t -> p i t", i=PACK)
+        words_hbm = out_1[0].rearrange("p t r -> p (t r)").bitcast(I32)
+
         x_sb = [sb.tile([P, PACK, PAD + T], F32, name="x%d" % z) for z in range(PASSES)]
         fa_sb = sb.tile([P, PASSES, PACK], F32)
         fb_sb = sb.tile([P, PASSES, PACK], F32)
@@ -51,72 +57,59 @@ def tile_mix_ahead_and_behind_pl_kernel(
         wa_plane = sb.tile([P, PASSES, N], U8, align_bytes=64)
         wb_plane = sb.tile([P, PASSES, N], U8, align_bytes=64)
         identity = sb.tile([P, P], F32)
+
+        widths = [count for z, first, count in STEPS]
+        peak = [sb.tile([P, PACK, w], F32, name="peak%d" % s) for s, w in enumerate(widths)]
+        diff = [sb.tile([P, PACK, w], F32, name="diff%d" % s) for s, w in enumerate(widths)]
+        rows = [sb.tile([P, 2, PACK, w], BF16, name="rows%d" % s) for s, w in enumerate(widths)]
+        packed = [
+            sb.tile([P, 2, w, PACK], BF16, name="packed%d" % s, align_bytes=64) for s, w in enumerate(widths)
+        ]
+        short = [sb.tile([P, PACK, TILE], F32, name="short%d" % s) for s in range(PASSES)]
+        codes, planes = {}, {}
+
+        acc = [ps.tile([P, N], F32, name="acc%d" % c) for c in range(TILES)]
+        dealt = [sb.tile([P, PACK, P], F32, name="dealt%d" % c) for c in range(TILES)]
+        turned = {}
+        y_sb = [sb.tile([P, PACK, TILE], F32, name="y_sb%d" % c) for c in range(TILES)]
+        y_bf = sb.tile([P, T, PACK], BF16, align_bytes=64)
+        y_codes = sb.tile([P, T], U32, align_bytes=64)
         y_plane = sb.tile([P, T], U8, align_bytes=64)
 
         def load_x(s, js=ALL):
-            c, z = steps[s]
+            z, first, count = STEPS[s]
             nc.sync.dma_start(
-                out=x_sb[z][:, js, PAD + c * TILE : PAD + (c + 1) * TILE],
-                in_=x_hbm[z][:, js, c * TILE : (c + 1) * TILE],
+                out=x_sb[z][:, js, PAD + first : PAD + first + count], in_=x_hbm[z][:, js, first : first + count]
             )
 
+        def load_factors(tile, factors):
+            nc.sync.dma_start(out=tile[:], in_=factors.rearrange("(z p j) o -> p z (j o)", z=PASSES, j=PACK))
+
         def load_plane(plane, scales):
-            for q in range(4):
+            for q in range(QUADRANTS):
                 nc.sync.dma_start(
                     out=plane[32 * q : 32 * q + 4, :, :].bitcast(I32),
                     in_=scales[:, 4 * q : 4 * q + 4, :].rearrange("z r n -> r z n").bitcast(I32),
                 )
 
-        for z in range(PASSES):
-            nc.vector.memset(x_sb[z][:, :, 0:PAD], 0.0)
-        for plane in (wa_plane, wb_plane):
-            nc.vector.memset(plane[:].bitcast(I32), 0)
-        make_identity(nc, identity[:])
-
-        for js in PAIRS:
-            load_x(0, js)
-        nc.sync.dma_start(out=fb_sb[:], in_=fb.rearrange("(z p j) o -> p z (j o)", z=PASSES, j=PACK))
-        nc.sync.dma_start(out=fa_sb[:], in_=fa.rearrange("(z p j) o -> p z (j o)", z=PASSES, j=PACK))
-        for s in range(1, len(steps) - PASSES):
-            load_x(s)
-        nc.sync.dma_start(out=wa_sb[:].bitcast(I32), in_=wa_words.rearrange("z p n r -> p z (n r)").bitcast(I32))
-        nc.sync.dma_start(out=wb_sb[:].bitcast(I32), in_=wb_words.rearrange("z p b -> p z b").bitcast(I32))
-        load_plane(wa_plane, wa_scales)
-        load_plane(wb_plane, wb_scales)
-        for s in range(len(steps) - PASSES, len(steps)):
-            load_x(s)
-
-        nc.scalar.activation(out=neg_fb[:], in_=fb_sb[:], func=ACT.Copy, scale=-1.0)
-
-        peak = [sb.tile([P, PACK, TILE], F32, name="peak%d" % s) for s in range(len(steps))]
-        diff = [sb.tile([P, PACK, TILE], F32, name="diff%d" % s) for s in range(len(steps))]
-        rows, packed, codes, planes = {}, {}, {}, {}
-        acc, y_t, y_ps = {}, {}, {}
+        def shifted(s, back, js):
+            z, first, count = STEPS[s]
+            return x_sb[z][:, js, PAD + first - back : PAD + first - back + count]
 
         def take_peak(s, js=ALL):
-            c, z = steps[s]
-            t0 = PAD + c * TILE
-            nc.vector.tensor_tensor(
-                out=peak[s][:, js, :],
-                in0=x_sb[z][:, js, t0 - 1 : t0 - 1 + TILE],
-                in1=x_sb[z][:, js, t0 - 2 : t0 - 2 + TILE],
-                op=ALU.max,
-            )
+            nc.vector.tensor_tensor(out=peak[s][:, js, :], in0=shifted(s, 1, js), in1=shifted(s, 2, js), op=ALU.max)
 
         def take_diff(s, js=ALL):
-            c, z = steps[s]
-            t0 = PAD + c * TILE
             nc.vector.tensor_tensor(
-                out=diff[s][:, js, :], in0=x_sb[z][:, js, t0 : t0 + TILE], in1=peak[s][:, js, :], op=ALU.subtract
+                out=diff[s][:, js, :], in0=shifted(s, 0, js), in1=peak[s][:, js, :], op=ALU.subtract
             )
 
         def scale_rows(s, side):
-            z = steps[s][1]
+            z = STEPS[s][0]
             clip, factor = ((ALU.max, fa_sb), (ALU.min, neg_fb))[side]
-            rows[s, side] = sb.tile([P, PACK, TILE], BF16, name="rows%d_%d" % (s, side))
             for j in range(PACK):
                 nc.vector.tensor_scalar(
-                    out=rows[s, side][:, j, :],
+                    out=rows[s][:, side, j, :],
                     in0=diff[s][:, j, :],
                     scalar1=0.0,
                     scalar2=factor[:, z, j : j + 1],
@@ -124,86 +117,78 @@ def tile_mix_ahead_and_behind_pl_kernel(
                     op1=ALU.mult,
                 )
 
-        short = [sb.tile([P, PACK, TILE], F32, name="short%d" % s) for s in range(SHARED)]
-
-        def clip_on_scalar(s):
+        def clip_behind_on_scalar(s):
             nc.scalar.activation(out=short[s][:], in_=diff[s][:], func=ACT.Relu, scale=-1.0)
 
-        def scale_rows_on_scalar(s):
-            z = steps[s][1]
-            rows[s, 1] = sb.tile([P, PACK, TILE], BF16, name="rows%d_1" % s)
+        def scale_behind_on_scalar(s):
+            z = STEPS[s][0]
             for j in range(PACK):
                 nc.scalar.activation(
-                    out=rows[s, 1][:, j, :], in_=short[s][:, j, :], func=ACT.Copy, scale=fb_sb[:, z, j : j + 1]
+                    out=rows[s][:, BEHIND, j, :], in_=short[s][:, j, :], func=ACT.Copy, scale=fb_sb[:, z, j : j + 1]
                 )
 
-        def interleave(s, side, copy):
-            packed[s, side] = sb.tile([P, TILE, PACK], BF16, name="packed%d_%d" % (s, side), align_bytes=64)
+        def interleave(s, sides, copy):
             copy(
-                out=packed[s, side][:].rearrange("p (c i) j -> p c j i", i=RUN),
-                in_=rows[s, side][:].rearrange("p j (c i) -> p c j i", i=RUN),
+                out=packed[s][:, sides, :, :].rearrange("p a (c i) j -> p a c j i", i=RUN),
+                in_=rows[s][:, sides, :, :].rearrange("p a j (c i) -> p a c j i", i=RUN),
             )
+
+        def one(side):
+            return slice(side, side + 1)
 
         def quantize(s, side):
-            codes[s, side] = sb.tile([P, TILE], U32, name="codes%d_%d" % (s, side), align_bytes=64)
-            planes[s, side] = sb.tile([P, TILE], U8, name="plane%d_%d" % (s, side), align_bytes=64)
+            z, first, count = STEPS[s]
+            words = sb.tile([P, count], U32, name="codes%d_%d" % (s, side), align_bytes=64)
+            plane = sb.tile([P, count], U8, name="plane%d_%d" % (s, side), align_bytes=64)
             nc.vector.quantize_mx(
-                out=codes[s, side][:].bitcast((E5M2, E4M3)[side]),
-                scales=planes[s, side][:],
-                in_=packed[s, side][:].rearrange("p t j -> p (t j)"),
+                out=words[:].bitcast((E5M2, E4M3)[side]),
+                scales=plane[:],
+                in_=packed[s][:, side, :, :].rearrange("p t j -> p (t j)"),
             )
+            for t0 in range(0, count, TILE):
+                codes[(first + t0) // TILE, z, side] = words[:, t0 : t0 + TILE]
+                planes[(first + t0) // TILE, z, side] = plane[:, t0 : t0 + TILE]
 
         def multiply(s):
-            c, z = steps[s]
-            if z == 0:
-                acc[c] = ps.tile([P, N], F32, name="acc%d" % c)
-            nc.tensor.matmul_mx(
-                out=acc[c][:],
-                lhsT=codes[s, 0][:].bitcast(E5M2),
-                lhsT_scale=planes[s, 0][:],
-                rhs=wa_sb[:, z, :].bitcast(E4M3),
-                rhs_scale=wa_plane[:, z, :],
-                start=(z == 0),
-                stop=False,
-            )
-            nc.tensor.matmul_mx(
-                out=acc[c][:],
-                lhsT=codes[s, 1][:].bitcast(E4M3),
-                lhsT_scale=planes[s, 1][:],
-                rhs=wb_sb[:, z, :].bitcast(E2M1),
-                rhs_scale=wb_plane[:, z, :],
-                start=False,
-                stop=(z == PASSES - 1),
-            )
+            z, first, count = STEPS[s]
+            for c in range(first // TILE, (first + count) // TILE):
+                nc.tensor.matmul_mx(
+                    out=acc[c][:],
+                    lhsT=codes[c, z, AHEAD].bitcast(E5M2),
+                    lhsT_scale=planes[c, z, AHEAD],
+                    rhs=wa_sb[:, z, :].bitcast(E4M3),
+                    rhs_scale=wa_plane[:, z, :],
+                    start=(z == 0),
+                    stop=False,
+                )
+                nc.tensor.matmul_mx(
+                    out=acc[c][:],
+                    lhsT=codes[c, z, BEHIND].bitcast(E4M3),
+                    lhsT_scale=planes[c, z, BEHIND],
+                    rhs=wb_sb[:, z, :].bitcast(E2M1),
+                    rhs_scale=wb_plane[:, z, :],
+                    start=False,
+                    stop=(z == PASSES - 1),
+                )
 
-        y_hbm = out_0.rearrange("(p i) t -> p i t", i=PACK)
-        y_sb = [sb.tile([P, PACK, TILE], F32, name="y_sb%d" % c) for c in range(TILES)]
-
-        def drain(c, pieces=(ALL,)):
-            y_t[c] = sb.tile([P, PACK, P], F32, name="y_t%d" % c)
-            dealt = acc[c][:].rearrange("t (p i) -> t i p", i=PACK)
-            for part in pieces:
-                nc.scalar.copy(out=y_t[c][:, part, :], in_=dealt[:, part, :])
+        def drain(c, copy, part=ALL):
+            copy(out=dealt[c][:, part, :], in_=acc[c][:].rearrange("t (p i) -> t i p", i=PACK)[:, part, :])
 
         def turn(c, part=ALL):
             count = part.stop - part.start
-            bank = ps.tile([P, count, TILE], F32, name="y_ps%d_%d" % (c, part.start), tag="turned", bufs=4)
+            bank = ps.tile([P, count, TILE], F32, name="turned%d_%d" % (c, part.start), tag="turned", bufs=TILES)
             for i in range(count):
-                nc.tensor.transpose(bank[:, i, :], y_t[c][:, part.start + i, :], identity[:])
-            y_ps[c, part.start] = bank
+                nc.tensor.transpose(bank[:, i, :], dealt[c][:, part.start + i, :], identity[:])
+            turned[c, part.start] = bank
 
         def store_result(c, copy, queue, part=ALL):
-            copy(out=y_sb[c][:, part, :], in_=y_ps[c, part.start][:])
+            copy(out=y_sb[c][:, part, :], in_=turned[c, part.start][:])
             queue.dma_start(out=y_hbm[:, part, c * TILE : (c + 1) * TILE], in_=y_sb[c][:, part, :])
 
-        y_bf = sb.tile([P, T, PACK], BF16, align_bytes=64)
-        y_codes = sb.tile([P, T], U32, align_bytes=64)
-        words_hbm = out_1[0].rearrange("p t r -> p (t r)").bitcast(I32)
-
-        def round_from_sbuf(c):
+        def round_result(c):
             nc.vector.tensor_copy(
-                out=y_bf[:, c * TILE : (c + 1) * TILE, :].rearrange("p (c i) j -> p c j i", i=RUN),
-                in_=y_sb[c][:].rearrange("p j (c i) -> p c j i", i=RUN),
+                out=y_bf[:, c * TILE : (c + 1) * TILE, :].rearrange("p (c r) i -> p c i r", r=RUN),
+                in_=y_sb[c][:].rearrange("p i (c r) -> p c i r", r=RUN),
             )
 
         def quantize_result(first, count):
@@ -219,73 +204,103 @@ def tile_mix_ahead_and_behind_pl_kernel(
             nc.sync.dma_start(out=words_hbm[:, tokens], in_=y_codes[:, tokens].bitcast(I32))
 
         def quantize_and_multiply(s):
-            quantize(s, 0)
-            quantize(s, 1)
+            quantize(s, AHEAD)
+            quantize(s, BEHIND)
             multiply(s)
+
+        for z in range(PASSES):
+            nc.vector.memset(x_sb[z][:, :, 0:PAD], 0.0)
+        for plane in (wa_plane, wb_plane):
+            nc.vector.memset(plane[:].bitcast(I32), 0)
+        make_identity(nc, identity[:])
+
+        for js in PAIRS:
+            load_x(0, js)
+        load_factors(fb_sb, fb)
+        load_factors(fa_sb, fa)
+        for s in (1, 2, 3):
+            load_x(s)
+        nc.sync.dma_start(out=wa_sb[:].bitcast(I32), in_=wa_words.rearrange("z p n r -> p z (n r)").bitcast(I32))
+        nc.sync.dma_start(out=wb_sb[:].bitcast(I32), in_=wb_words.rearrange("z p b -> p z b").bitcast(I32))
+        load_plane(wa_plane, wa_scales)
+        load_plane(wb_plane, wb_scales)
+        for s in (4, 5):
+            load_x(s)
+        nc.scalar.activation(out=neg_fb[:], in_=fb_sb[:], func=ACT.Copy, scale=-1.0)
 
         for js in PAIRS:
             take_peak(0, js)
         for js in PAIRS:
             take_diff(0, js)
-        for s in range(last - 1):
-            if s > 0:
-                take_diff(s)
-            take_peak(s + 1)
-            if s == 5:
-                drain(0)
-                turn(0)
-                quantize_and_multiply(3)
-            if s < SHARED:
-                clip_on_scalar(s)
-                if s > 0:
-                    interleave(s - 1, 1, nc.scalar.copy)
-                scale_rows_on_scalar(s)
-            scale_rows(s, 0)
-            interleave(s, 0, nc.scalar.copy)
-            if s >= SHARED:
-                scale_rows(s, 1)
-            if s >= SHARED - 1:
-                interleave(s, 1, nc.scalar.copy)
-            if s == 5:
-                quantize_and_multiply(4)
-            elif s >= 2:
-                quantize_and_multiply(s - 2)
-        store_result(0, nc.scalar.copy, nc.sync)
-        drain(1)
+        clip_behind_on_scalar(0)
+        scale_behind_on_scalar(0)
+        take_peak(1)
+        scale_rows(0, AHEAD)
+        take_diff(1)
+        clip_behind_on_scalar(1)
+        interleave(0, BOTH, nc.scalar.copy)
+        scale_behind_on_scalar(1)
+        take_peak(2)
+        scale_rows(1, AHEAD)
+        interleave(1, BOTH, nc.scalar.copy)
 
-        for s in (last - 1, last):
+        take_diff(2)
+        take_peak(3)
+        scale_rows(2, AHEAD)
+        interleave(2, one(AHEAD), nc.scalar.copy)
+        quantize_and_multiply(0)
+        scale_rows(2, BEHIND)
+        interleave(2, one(BEHIND), nc.scalar.copy)
+        quantize_and_multiply(1)
+        drain(0, nc.scalar.copy)
+
+        for s in (3, 4):
             take_diff(s)
-            if s < last:
-                take_peak(s + 1)
-            quantize(s - 1, 0)
-            scale_rows(s, 0)
-            interleave(s, 0, nc.scalar.copy)
-            quantize(s - 1, 1)
+            quantize(s - 1, AHEAD)
+            scale_rows(s, AHEAD)
+            interleave(s, one(AHEAD), nc.scalar.copy)
+            take_peak(s + 1)
+            quantize(s - 1, BEHIND)
             multiply(s - 1)
-            turn(s - 5)
-            scale_rows(s, 1)
-            if s < last:
-                interleave(s, 1, nc.scalar.copy)
-                drain(2)
-        interleave(last, 1, nc.vector.tensor_copy)
-        quantize_and_multiply(last)
-        store_result(1, nc.scalar.copy, nc.sync)
+            if s == 3:
+                turn(0)
+            else:
+                store_result(0, nc.scalar.copy, nc.sync)
+            scale_rows(s, BEHIND)
+            interleave(s, one(BEHIND), nc.scalar.copy)
+        for c in (1, 2):
+            drain(c, nc.scalar.copy)
+
+        take_diff(5)
+        quantize(4, AHEAD)
+        scale_rows(5, AHEAD)
+        quantize(4, BEHIND)
+        multiply(4)
+        turn(1)
+        scale_rows(5, BEHIND)
+        for side in (AHEAD, BEHIND):
+            interleave(5, one(side), nc.vector.tensor_copy)
+        quantize_and_multiply(5)
+        turn(2)
+        for c in (1, 2):
+            store_result(c, nc.scalar.copy, nc.sync)
+
         for c in (0, 1):
-            round_from_sbuf(c)
-        store_result(2, nc.scalar.copy, nc.sync)
+            round_result(c)
+        for i in range(PACK):
+            drain(3, nc.vector.tensor_copy, slice(i, i + 1))
+        for part in PAIRS:
+            turn(3, part)
         quantize_result(0, 2)
-        round_from_sbuf(2)
+        round_result(2)
+        store_result(3, nc.scalar.copy, nc.scalar, PAIRS[0])
+        store_result(3, nc.vector.tensor_copy, nc.sync, PAIRS[1])
         quantize_result(2, 1)
         store_words(0, 3)
-        drain(TILES - 1, [slice(i, i + 1) for i in range(PACK)])
-        for part in PAIRS:
-            turn(TILES - 1, part)
-        store_result(TILES - 1, nc.scalar.copy, nc.scalar, PAIRS[0])
-        store_result(TILES - 1, nc.vector.tensor_copy, nc.sync, PAIRS[1])
-        round_from_sbuf(TILES - 1)
-        quantize_result(TILES - 1, 1)
-        store_words(TILES - 1, 1)
-        for q in range(4):
+        round_result(3)
+        quantize_result(3, 1)
+        store_words(3, 1)
+        for q in range(QUADRANTS):
             queue = (nc.sync, nc.scalar)[q % 2]
             queue.dma_start(
                 out=out_2[0][4 * q : 4 * q + 4, :].bitcast(I32),

@@ -23,7 +23,8 @@ PASSES = K // (P * PACK)
 TILE = 128
 TILES = T // TILE
 QUADRANTS = 4
-PAD = 8
+BLOCK = 8
+PAD = BLOCK
 RUN = 4
 AHEAD, BEHIND = 0, 1
 BOTH = slice(0, 2)
@@ -49,8 +50,8 @@ def tile_mix_ahead_and_behind_pl_kernel(
         words_hbm = out_1[0].rearrange("p t r -> p (t r)").bitcast(I32)
 
         x_sb = [sb.tile([P, PACK, PAD + T], F32, name="x%d" % z) for z in range(PASSES)]
-        fa_sb = sb.tile([P, PASSES, PACK], F32)
-        fb_sb = sb.tile([P, PASSES, PACK], F32)
+        fa_sb = sb.tile([P, PASSES, BLOCK], F32)
+        fb_sb = sb.tile([P, PASSES, BLOCK], F32)
         neg_fb = sb.tile([P, PASSES, PACK], F32)
         wa_sb = sb.tile([P, PASSES, N], U32, align_bytes=64)
         wb_sb = sb.tile([P, PASSES, 2 * N], U8, align_bytes=64)
@@ -66,7 +67,6 @@ def tile_mix_ahead_and_behind_pl_kernel(
             sb.tile([P, 2, w, PACK], BF16, name="packed%d" % s, align_bytes=64) for s, w in enumerate(widths)
         ]
         short = [sb.tile([P, PACK, TILE], F32, name="short%d" % s) for s in range(PASSES)]
-        codes, planes = {}, {}
 
         acc = [ps.tile([P, N], F32, name="acc%d" % c) for c in range(TILES)]
         dealt = [sb.tile([P, PACK, P], F32, name="dealt%d" % c) for c in range(TILES)]
@@ -83,7 +83,7 @@ def tile_mix_ahead_and_behind_pl_kernel(
             )
 
         def load_factors(tile, factors):
-            nc.sync.dma_start(out=tile[:], in_=factors.rearrange("(z p j) o -> p z (j o)", z=PASSES, j=PACK))
+            nc.sync.dma_start(out=tile[:, :, ALL], in_=factors.rearrange("(z p j) o -> p z (j o)", z=PASSES, j=PACK))
 
         def load_plane(plane, scales):
             for q in range(QUADRANTS):
@@ -127,48 +127,40 @@ def tile_mix_ahead_and_behind_pl_kernel(
                     out=rows[s][:, BEHIND, j, :], in_=short[s][:, j, :], func=ACT.Copy, scale=fb_sb[:, z, j : j + 1]
                 )
 
-        def interleave(s, sides, copy):
-            copy(
-                out=packed[s][:, sides, :, :].rearrange("p a (c i) j -> p a c j i", i=RUN),
-                in_=rows[s][:, sides, :, :].rearrange("p a j (c i) -> p a c j i", i=RUN),
+        def interleave_on_scalar(s, sides):
+            nc.scalar.copy(
+                out=packed[s][:, sides, :, :].rearrange("p a (c r) j -> p a c j r", r=RUN),
+                in_=rows[s][:, sides, :, :].rearrange("p a j (c r) -> p a c j r", r=RUN),
             )
+
+        def interleave_on_vector(s, side):
+            nc.vector.tensor_copy(out=packed[s][:, side, :, :], in_=rows[s][:, side, :, :].rearrange("p j t -> p t j"))
 
         def one(side):
             return slice(side, side + 1)
 
-        def quantize(s, side):
+        def multiply(s, side):
             z, first, count = STEPS[s]
-            words = sb.tile([P, count], U32, name="codes%d_%d" % (s, side), align_bytes=64)
+            act_format, weights, weight_plane = (
+                (E5M2, wa_sb[:, z, :].bitcast(E4M3), wa_plane),
+                (E4M3, wb_sb[:, z, :].bitcast(E2M1), wb_plane),
+            )[side]
+            codes = sb.tile([P, count], U32, name="codes%d_%d" % (s, side), align_bytes=64)
             plane = sb.tile([P, count], U8, name="plane%d_%d" % (s, side), align_bytes=64)
             nc.vector.quantize_mx(
-                out=words[:].bitcast((E5M2, E4M3)[side]),
+                out=codes[:].bitcast(act_format),
                 scales=plane[:],
                 in_=packed[s][:, side, :, :].rearrange("p t j -> p (t j)"),
             )
             for t0 in range(0, count, TILE):
-                codes[(first + t0) // TILE, z, side] = words[:, t0 : t0 + TILE]
-                planes[(first + t0) // TILE, z, side] = plane[:, t0 : t0 + TILE]
-
-        def multiply(s):
-            z, first, count = STEPS[s]
-            for c in range(first // TILE, (first + count) // TILE):
                 nc.tensor.matmul_mx(
-                    out=acc[c][:],
-                    lhsT=codes[c, z, AHEAD].bitcast(E5M2),
-                    lhsT_scale=planes[c, z, AHEAD],
-                    rhs=wa_sb[:, z, :].bitcast(E4M3),
-                    rhs_scale=wa_plane[:, z, :],
-                    start=(z == 0),
-                    stop=False,
-                )
-                nc.tensor.matmul_mx(
-                    out=acc[c][:],
-                    lhsT=codes[c, z, BEHIND].bitcast(E4M3),
-                    lhsT_scale=planes[c, z, BEHIND],
-                    rhs=wb_sb[:, z, :].bitcast(E2M1),
-                    rhs_scale=wb_plane[:, z, :],
-                    start=False,
-                    stop=(z == PASSES - 1),
+                    out=acc[(first + t0) // TILE][:],
+                    lhsT=codes[:, t0 : t0 + TILE].bitcast(act_format),
+                    lhsT_scale=plane[:, t0 : t0 + TILE],
+                    rhs=weights,
+                    rhs_scale=weight_plane[:, z, :],
+                    start=(z == 0 and side == AHEAD),
+                    stop=(z == PASSES - 1 and side == BEHIND),
                 )
 
         def drain(c, copy, part=ALL):
@@ -187,8 +179,7 @@ def tile_mix_ahead_and_behind_pl_kernel(
 
         def round_result(c):
             nc.vector.tensor_copy(
-                out=y_bf[:, c * TILE : (c + 1) * TILE, :].rearrange("p (c r) i -> p c i r", r=RUN),
-                in_=y_sb[c][:].rearrange("p i (c r) -> p c i r", r=RUN),
+                out=y_bf[:, c * TILE : (c + 1) * TILE, :], in_=y_sb[c][:].rearrange("p i t -> p t i")
             )
 
         def quantize_result(first, count):
@@ -203,10 +194,9 @@ def tile_mix_ahead_and_behind_pl_kernel(
             tokens = slice(first * TILE, (first + count) * TILE)
             nc.sync.dma_start(out=words_hbm[:, tokens], in_=y_codes[:, tokens].bitcast(I32))
 
-        def quantize_and_multiply(s):
-            quantize(s, AHEAD)
-            quantize(s, BEHIND)
-            multiply(s)
+        def multiply_both(s):
+            multiply(s, AHEAD)
+            multiply(s, BEHIND)
 
         for z in range(PASSES):
             nc.vector.memset(x_sb[z][:, :, 0:PAD], 0.0)
@@ -216,9 +206,10 @@ def tile_mix_ahead_and_behind_pl_kernel(
 
         for js in PAIRS:
             load_x(0, js)
-        load_factors(fb_sb, fb)
+        load_x(1)
         load_factors(fa_sb, fa)
-        for s in (1, 2, 3):
+        load_factors(fb_sb, fb)
+        for s in (2, 3):
             load_x(s)
         nc.sync.dma_start(out=wa_sb[:].bitcast(I32), in_=wa_words.rearrange("z p n r -> p z (n r)").bitcast(I32))
         nc.sync.dma_start(out=wb_sb[:].bitcast(I32), in_=wb_words.rearrange("z p b -> p z b").bitcast(I32))
@@ -226,7 +217,6 @@ def tile_mix_ahead_and_behind_pl_kernel(
         load_plane(wb_plane, wb_scales)
         for s in (4, 5):
             load_x(s)
-        nc.scalar.activation(out=neg_fb[:], in_=fb_sb[:], func=ACT.Copy, scale=-1.0)
 
         for js in PAIRS:
             take_peak(0, js)
@@ -234,54 +224,53 @@ def tile_mix_ahead_and_behind_pl_kernel(
             take_diff(0, js)
         clip_behind_on_scalar(0)
         scale_behind_on_scalar(0)
+        nc.scalar.activation(out=neg_fb[:], in_=fb_sb[:, :, ALL], func=ACT.Copy, scale=-1.0)
         take_peak(1)
         scale_rows(0, AHEAD)
         take_diff(1)
         clip_behind_on_scalar(1)
-        interleave(0, BOTH, nc.scalar.copy)
+        interleave_on_scalar(0, BOTH)
         scale_behind_on_scalar(1)
         take_peak(2)
         scale_rows(1, AHEAD)
-        interleave(1, BOTH, nc.scalar.copy)
+        interleave_on_scalar(1, BOTH)
 
         take_diff(2)
         take_peak(3)
         scale_rows(2, AHEAD)
-        interleave(2, one(AHEAD), nc.scalar.copy)
-        quantize_and_multiply(0)
+        interleave_on_scalar(2, one(AHEAD))
+        multiply_both(0)
         scale_rows(2, BEHIND)
-        interleave(2, one(BEHIND), nc.scalar.copy)
-        quantize_and_multiply(1)
+        interleave_on_scalar(2, one(BEHIND))
+        multiply_both(1)
         drain(0, nc.scalar.copy)
 
         for s in (3, 4):
             take_diff(s)
-            quantize(s - 1, AHEAD)
+            multiply(s - 1, AHEAD)
             scale_rows(s, AHEAD)
-            interleave(s, one(AHEAD), nc.scalar.copy)
+            interleave_on_scalar(s, one(AHEAD))
             take_peak(s + 1)
-            quantize(s - 1, BEHIND)
-            multiply(s - 1)
+            multiply(s - 1, BEHIND)
             if s == 3:
                 turn(0)
             else:
                 store_result(0, nc.scalar.copy, nc.sync)
             scale_rows(s, BEHIND)
-            interleave(s, one(BEHIND), nc.scalar.copy)
+            interleave_on_scalar(s, one(BEHIND))
         for c in (1, 2):
             drain(c, nc.scalar.copy)
 
         take_diff(5)
-        quantize(4, AHEAD)
+        multiply(4, AHEAD)
         scale_rows(5, AHEAD)
-        quantize(4, BEHIND)
-        multiply(4)
-        turn(1)
+        multiply(4, BEHIND)
+        for c in (1, 2):
+            turn(c)
         scale_rows(5, BEHIND)
         for side in (AHEAD, BEHIND):
-            interleave(5, one(side), nc.vector.tensor_copy)
-        quantize_and_multiply(5)
-        turn(2)
+            interleave_on_vector(5, side)
+        multiply_both(5)
         for c in (1, 2):
             store_result(c, nc.scalar.copy, nc.sync)
 

from contextlib import ExitStack

import concourse.mybir as mybir
from concourse.masks import make_identity

K, T, N = 1024, 512, 512
FLOPS = 2 * 2 * K * T * N

F32 = mybir.dt.float32
BF16 = mybir.dt.bfloat16
I32 = mybir.dt.int32
U32 = mybir.dt.uint32
U8 = mybir.dt.uint8
E4M3 = mybir.dt.float8_e4m3fn_x4
E5M2 = mybir.dt.float8_e5m2_x4
E2M1 = mybir.dt.float4_e2m1fn_x4
ALU = mybir.AluOpType
ACT = mybir.ActivationFunctionType

P = 128
PACK = 4
PASSES = K // (P * PACK)
TILE = 128
TILES = T // TILE
QUADRANTS = 4
BLOCK = 8
PAD = BLOCK
RUN = 4
AHEAD, BEHIND = 0, 1
BOTH = slice(0, 2)
ALL = slice(0, PACK)
PAIRS = (slice(0, 2), slice(2, 4))

RANGES = ((0, TILE), (TILE, 2 * TILE), (3 * TILE, TILE))
STEPS = [(z, first, count) for first, count in RANGES for z in range(PASSES)]


def tile_mix_ahead_and_behind_pl_kernel(
    tc, xf, fa, fb, wa_words, wa_scales, wb_words, wb_scales, out_0, out_1, out_2
):
    nc = tc.nc

    with ExitStack() as ctx:
        sb = ctx.enter_context(tc.tile_pool(name="sb", bufs=1))
        ps = ctx.enter_context(tc.psum_pool(name="ps", bufs=1))
        ctx.enter_context(tc.manual_schedule())

        x_hbm = xf.rearrange("(z p j) t -> z p j t", z=PASSES, j=PACK)
        y_hbm = out_0.rearrange("(p i) t -> p i t", i=PACK)
        words_hbm = out_1[0].rearrange("p t r -> p (t r)").bitcast(I32)

        x_sb = [sb.tile([P, PACK, PAD + T], F32, name="x%d" % z) for z in range(PASSES)]
        fa_sb = sb.tile([P, PASSES, BLOCK], F32)
        fb_sb = sb.tile([P, PASSES, BLOCK], F32)
        neg_fb = sb.tile([P, PASSES, PACK], F32)
        wa_sb = sb.tile([P, PASSES, N], U32, align_bytes=64)
        wb_sb = sb.tile([P, PASSES, 2 * N], U8, align_bytes=64)
        wa_plane = sb.tile([P, PASSES, N], U8, align_bytes=64)
        wb_plane = sb.tile([P, PASSES, N], U8, align_bytes=64)
        identity = sb.tile([P, P], F32)

        widths = [count for z, first, count in STEPS]
        peak = [sb.tile([P, PACK, w], F32, name="peak%d" % s) for s, w in enumerate(widths)]
        diff = [sb.tile([P, PACK, w], F32, name="diff%d" % s) for s, w in enumerate(widths)]
        rows = [sb.tile([P, 2, PACK, w], BF16, name="rows%d" % s) for s, w in enumerate(widths)]
        packed = [
            sb.tile([P, 2, w, PACK], BF16, name="packed%d" % s, align_bytes=64) for s, w in enumerate(widths)
        ]
        short = [sb.tile([P, PACK, TILE], F32, name="short%d" % s) for s in range(PASSES)]

        acc = [ps.tile([P, N], F32, name="acc%d" % c) for c in range(TILES)]
        dealt = [sb.tile([P, PACK, P], F32, name="dealt%d" % c) for c in range(TILES)]
        turned = {}
        y_sb = [sb.tile([P, PACK, TILE], F32, name="y_sb%d" % c) for c in range(TILES)]
        y_bf = sb.tile([P, T, PACK], BF16, align_bytes=64)
        y_codes = sb.tile([P, T], U32, align_bytes=64)
        y_plane = sb.tile([P, T], U8, align_bytes=64)

        def load_x(s, js=ALL):
            z, first, count = STEPS[s]
            nc.sync.dma_start(
                out=x_sb[z][:, js, PAD + first : PAD + first + count], in_=x_hbm[z][:, js, first : first + count]
            )

        def load_factors(tile, factors):
            nc.sync.dma_start(out=tile[:, :, ALL], in_=factors.rearrange("(z p j) o -> p z (j o)", z=PASSES, j=PACK))

        def load_plane(plane, scales):
            for q in range(QUADRANTS):
                nc.sync.dma_start(
                    out=plane[32 * q : 32 * q + 4, :, :].bitcast(I32),
                    in_=scales[:, 4 * q : 4 * q + 4, :].rearrange("z r n -> r z n").bitcast(I32),
                )

        def shifted(s, back, js):
            z, first, count = STEPS[s]
            return x_sb[z][:, js, PAD + first - back : PAD + first - back + count]

        def take_peak(s, js=ALL):
            nc.vector.tensor_tensor(out=peak[s][:, js, :], in0=shifted(s, 1, js), in1=shifted(s, 2, js), op=ALU.max)

        def take_diff(s, js=ALL):
            nc.vector.tensor_tensor(
                out=diff[s][:, js, :], in0=shifted(s, 0, js), in1=peak[s][:, js, :], op=ALU.subtract
            )

        def scale_rows(s, side):
            z = STEPS[s][0]
            clip, factor = ((ALU.max, fa_sb), (ALU.min, neg_fb))[side]
            for j in range(PACK):
                nc.vector.tensor_scalar(
                    out=rows[s][:, side, j, :],
                    in0=diff[s][:, j, :],
                    scalar1=0.0,
                    scalar2=factor[:, z, j : j + 1],
                    op0=clip,
                    op1=ALU.mult,
                )

        def clip_behind_on_scalar(s):
            nc.scalar.activation(out=short[s][:], in_=diff[s][:], func=ACT.Relu, scale=-1.0)

        def scale_behind_on_scalar(s):
            z = STEPS[s][0]
            for j in range(PACK):
                nc.scalar.activation(
                    out=rows[s][:, BEHIND, j, :], in_=short[s][:, j, :], func=ACT.Copy, scale=fb_sb[:, z, j : j + 1]
                )

        def interleave_on_scalar(s, sides):
            nc.scalar.copy(
                out=packed[s][:, sides, :, :].rearrange("p a (c r) j -> p a c j r", r=RUN),
                in_=rows[s][:, sides, :, :].rearrange("p a j (c r) -> p a c j r", r=RUN),
            )

        def interleave_on_vector(s, side):
            nc.vector.tensor_copy(out=packed[s][:, side, :, :], in_=rows[s][:, side, :, :].rearrange("p j t -> p t j"))

        def one(side):
            return slice(side, side + 1)

        def multiply(s, side):
            z, first, count = STEPS[s]
            act_format, weights, weight_plane = (
                (E5M2, wa_sb[:, z, :].bitcast(E4M3), wa_plane),
                (E4M3, wb_sb[:, z, :].bitcast(E2M1), wb_plane),
            )[side]
            codes = sb.tile([P, count], U32, name="codes%d_%d" % (s, side), align_bytes=64)
            plane = sb.tile([P, count], U8, name="plane%d_%d" % (s, side), align_bytes=64)
            nc.vector.quantize_mx(
                out=codes[:].bitcast(act_format),
                scales=plane[:],
                in_=packed[s][:, side, :, :].rearrange("p t j -> p (t j)"),
            )
            for t0 in range(0, count, TILE):
                nc.tensor.matmul_mx(
                    out=acc[(first + t0) // TILE][:],
                    lhsT=codes[:, t0 : t0 + TILE].bitcast(act_format),
                    lhsT_scale=plane[:, t0 : t0 + TILE],
                    rhs=weights,
                    rhs_scale=weight_plane[:, z, :],
                    start=(z == 0 and side == AHEAD),
                    stop=(z == PASSES - 1 and side == BEHIND),
                )

        def drain(c, copy, part=ALL):
            copy(out=dealt[c][:, part, :], in_=acc[c][:].rearrange("t (p i) -> t i p", i=PACK)[:, part, :])

        def turn(c, part=ALL):
            count = part.stop - part.start
            bank = ps.tile([P, count, TILE], F32, name="turned%d_%d" % (c, part.start), tag="turned", bufs=TILES)
            for i in range(count):
                nc.tensor.transpose(bank[:, i, :], dealt[c][:, part.start + i, :], identity[:])
            turned[c, part.start] = bank

        def store_result(c, copy, queue, part=ALL):
            copy(out=y_sb[c][:, part, :], in_=turned[c, part.start][:])
            queue.dma_start(out=y_hbm[:, part, c * TILE : (c + 1) * TILE], in_=y_sb[c][:, part, :])

        def round_result(c):
            nc.vector.tensor_copy(
                out=y_bf[:, c * TILE : (c + 1) * TILE, :], in_=y_sb[c][:].rearrange("p i t -> p t i")
            )

        def quantize_result(first, count):
            tokens = slice(first * TILE, (first + count) * TILE)
            nc.vector.quantize_mx(
                out=y_codes[:, tokens].bitcast(E4M3),
                scales=y_plane[:, tokens],
                in_=y_bf[:, tokens, :].rearrange("p t i -> p (t i)"),
            )

        def store_words(first, count):
            tokens = slice(first * TILE, (first + count) * TILE)
            nc.sync.dma_start(out=words_hbm[:, tokens], in_=y_codes[:, tokens].bitcast(I32))

        def multiply_both(s):
            multiply(s, AHEAD)
            multiply(s, BEHIND)

        for z in range(PASSES):
            nc.vector.memset(x_sb[z][:, :, 0:PAD], 0.0)
        for plane in (wa_plane, wb_plane):
            nc.vector.memset(plane[:].bitcast(I32), 0)
        make_identity(nc, identity[:])

        for js in PAIRS:
            load_x(0, js)
        load_x(1)
        load_factors(fa_sb, fa)
        load_factors(fb_sb, fb)
        for s in (2, 3):
            load_x(s)
        nc.sync.dma_start(out=wa_sb[:].bitcast(I32), in_=wa_words.rearrange("z p n r -> p z (n r)").bitcast(I32))
        nc.sync.dma_start(out=wb_sb[:].bitcast(I32), in_=wb_words.rearrange("z p b -> p z b").bitcast(I32))
        load_plane(wa_plane, wa_scales)
        load_plane(wb_plane, wb_scales)
        for s in (4, 5):
            load_x(s)

        for js in PAIRS:
            take_peak(0, js)
        for js in PAIRS:
            take_diff(0, js)
        clip_behind_on_scalar(0)
        scale_behind_on_scalar(0)
        nc.scalar.activation(out=neg_fb[:], in_=fb_sb[:, :, ALL], func=ACT.Copy, scale=-1.0)
        take_peak(1)
        scale_rows(0, AHEAD)
        take_diff(1)
        clip_behind_on_scalar(1)
        interleave_on_scalar(0, BOTH)
        scale_behind_on_scalar(1)
        take_peak(2)
        scale_rows(1, AHEAD)
        interleave_on_scalar(1, BOTH)

        take_diff(2)
        take_peak(3)
        scale_rows(2, AHEAD)
        interleave_on_scalar(2, one(AHEAD))
        multiply_both(0)
        scale_rows(2, BEHIND)
        interleave_on_scalar(2, one(BEHIND))
        multiply_both(1)
        drain(0, nc.scalar.copy)

        for s in (3, 4):
            take_diff(s)
            multiply(s - 1, AHEAD)
            scale_rows(s, AHEAD)
            interleave_on_scalar(s, one(AHEAD))
            take_peak(s + 1)
            multiply(s - 1, BEHIND)
            if s == 3:
                turn(0)
            else:
                store_result(0, nc.scalar.copy, nc.sync)
            scale_rows(s, BEHIND)
            interleave_on_scalar(s, one(BEHIND))
        for c in (1, 2):
            drain(c, nc.scalar.copy)

        take_diff(5)
        multiply(4, AHEAD)
        scale_rows(5, AHEAD)
        multiply(4, BEHIND)
        for c in (1, 2):
            turn(c)
        scale_rows(5, BEHIND)
        for side in (AHEAD, BEHIND):
            interleave_on_vector(5, side)
        multiply_both(5)
        for c in (1, 2):
            store_result(c, nc.scalar.copy, nc.sync)

        for c in (0, 1):
            round_result(c)
        for i in range(PACK):
            drain(3, nc.vector.tensor_copy, slice(i, i + 1))
        for part in PAIRS:
            turn(3, part)
        quantize_result(0, 2)
        round_result(2)
        store_result(3, nc.scalar.copy, nc.scalar, PAIRS[0])
        store_result(3, nc.vector.tensor_copy, nc.sync, PAIRS[1])
        quantize_result(2, 1)
        store_words(0, 3)
        round_result(3)
        quantize_result(3, 1)
        store_words(3, 1)
        for q in range(QUADRANTS):
            queue = (nc.sync, nc.scalar)[q % 2]
            queue.dma_start(
                out=out_2[0][4 * q : 4 * q + 4, :].bitcast(I32),
                in_=y_plane[32 * q : 32 * q + 4, :].bitcast(I32),
            )
